import numpy as np
import ml_dtypes


def mxq(x, axis, fmt="e4m3"):
    dtype, down = {"e4m3": (ml_dtypes.float8_e4m3fn, 7), "e5m2": (ml_dtypes.float8_e5m2, 14)}[fmt]
    v = np.moveaxis(np.asarray(x, np.float32).astype(ml_dtypes.bfloat16).astype(np.float64), axis, -1)
    blocks = v.reshape(v.shape[:-1] + (-1, 32))
    amax = np.abs(blocks).max(-1, keepdims=True)
    byte = np.maximum(np.where(amax > 0, np.frexp(amax)[1] - 1 + 127, 0) - down, 1)
    scale = np.exp2(byte - 127.0)
    codes = (blocks / scale).astype(np.float32).astype(dtype).astype(np.float64)
    return np.moveaxis((codes * scale).reshape(v.shape), -1, axis)


WIDE = False


def mx_kscale(k):
    if not WIDE:
        return np.ones(k)
    levels = np.array([10, -10, 5, -5, 0])
    if k % 512:
        return np.exp2(np.random.permutation(np.resize(levels, k // 32))).repeat(32)
    a = np.empty((k // 512, 16))
    for p in range(k // 512):
        a[p, :8] = np.random.permutation(np.resize(levels, 8))
        for g in range(8):
            far = levels[np.abs(levels - a[p, g]) >= 10]
            a[p, g + 8] = far[np.random.randint(len(far))]
    return np.exp2(a.ravel()).repeat(32)


def f64(x):
    return np.asarray(x).astype(np.float64)


def striped(idx):
    return np.tile(np.asarray(idx).reshape(-1, 16).T, (8, 1)).astype(np.uint16)


def unstriped(offs):
    return offs[:16].T.reshape(-1).astype(np.int64)


E2M1 = np.array([0.0, 0.5, 1.0, 1.5, 2.0, 3.0, 4.0, 6.0, -0.0, -0.5, -1.0, -1.5, -2.0, -3.0, -4.0, -6.0])


def pack_weight(w, fmt):
    k, n = w.shape
    w = f64(np.asarray(w, np.float32).astype(ml_dtypes.bfloat16)).reshape(k // 32, 32, n)
    amax = np.abs(w).max(1)
    if fmt == "e4m3":
        byte = np.frexp(amax)[1] - 1 + 127 - 7
    else:
        mant, ex = np.frexp(amax / 6.0)
        byte = np.where(mant > 0.5, ex, ex - 1) + 127
    byte = np.clip(np.where(amax > 0, byte, 1), 1, 254)
    scaled = (w * np.exp2(127.0 - byte)[:, None, :]).reshape(k, n).astype(np.float32)
    by_word = np.ascontiguousarray(scaled.reshape(k // 512, 128, 4, n).transpose(0, 1, 3, 2))
    if fmt == "e4m3":
        words = by_word.astype(ml_dtypes.float8_e4m3fn).view(np.uint8)
    else:
        c = by_word.astype(ml_dtypes.float4_e2m1fn).view(np.uint8) & 0xF
        words = (c[..., 0::2] | (c[..., 1::2] << 4)).reshape(k // 512, 128, 2 * n)
    return np.ascontiguousarray(words), np.ascontiguousarray(byte.astype(np.uint8).reshape(k // 512, 16, n))


def unpack_weight(words, scales, fmt):
    g, _, n = scales.shape
    words = np.ascontiguousarray(words).reshape(g, 128, n, -1)
    if fmt == "e4m3":
        vals = words.view(ml_dtypes.float8_e4m3fn).astype(np.float64)
    else:
        nib = np.empty((g, 128, n, 4), np.uint8)
        nib[..., 0::2] = words & 0xF
        nib[..., 1::2] = words >> 4
        vals = E2M1[nib]
    vals = vals * np.repeat(np.exp2(scales.astype(np.float64) - 127.0), 8, axis=1)[..., None]
    return vals.transpose(0, 1, 3, 2).reshape(g * 512, n)


def bf(x):
    return np.asarray(x, np.float32).astype(ml_dtypes.bfloat16)


def planes(Y):
    r, m = Y.shape
    b = f64(bf(Y)).reshape(r // 32, 32, m)
    amax = np.abs(b).max(1)
    byte = np.clip(np.where(amax > 0, np.frexp(amax)[1] - 1 + 127 - 7, 1), 1, 254)
    codes = (b * np.exp2(127.0 - byte)[:, None, :]).reshape(r, m).astype(np.float32).astype(ml_dtypes.float8_e4m3fn).view(np.uint8)
    words = codes.reshape(r // 512, 128, 4, m).transpose(0, 1, 3, 2)
    return np.ascontiguousarray(words), np.ascontiguousarray(byte.astype(np.uint8).reshape(r // 512, 16, m))


B, N, T, D, NQ = 1, 512, 2048, 1024, 512


def setup_inputs():
    n = np.random.standard_normal
    idx = np.sort(np.random.permutation(T)[:B * N].reshape(B, N), axis=1).reshape(-1)
    s = mx_kscale(D)[:, None]
    kp = pack_weight(n((D, T)) / s, "e2m1")
    return {
        "qT": (n((B, D, NQ)) * s * (1.00 / np.sqrt(D))).astype(np.float32),
        "k_words": np.ascontiguousarray(kp[0].reshape(1, 2, 128, T, 2).transpose(0, 2, 3, 1, 4)).reshape(1, 128, T, 4),
        "k_scales": kp[1],
        "offs": striped(idx),
    }


def reference(qT, k_words, k_scales, offs):
    idx = unstriped(offs)
    pick = lambda x, which: x[:, which].reshape(x.shape[0], B, -1).transpose(1, 0, 2)
    k = unpack_weight(k_words.reshape(1, 128, T, 2, 2).transpose(0, 3, 1, 2, 4).reshape(2, 128, 2 * T), k_scales, "e2m1")
    kg = pick(k, idx)
    qq = mxq(f64(qT), 1, "e4m3")
    a = kg.transpose(0, 2, 1) @ qq
    y = np.square(np.maximum(a, 0.0))
    Y = y[0]
    words, scales = planes(Y)
    return Y, words, scales

@@ -1,0 +1,185 @@
+from contextlib import ExitStack
+
+import concourse.mybir as mybir
+
+F32 = mybir.dt.float32
+BF16 = mybir.dt.bfloat16
+I32 = mybir.dt.int32
+U32 = mybir.dt.uint32
+U16 = mybir.dt.uint16
+U8 = mybir.dt.uint8
+FP8X4 = mybir.dt.float8_e4m3fn_x4
+FP4X4 = mybir.dt.float4_e2m1fn_x4
+ACT = mybir.ActivationFunctionType
+ALU = mybir.AluOpType
+
+P = 128
+PACK = 4
+PASSES = 2
+T = 2048
+SLOTS = 512
+NQ = 512
+HALF = 256
+CHUNK = 128
+FLOPS = 2 * SLOTS * NQ * 1024
+
+
+def interleave_views(dst, src):
+    return (
+        dst.rearrange("p (c i) t -> p c t i", i=4),
+        src.rearrange("p t (c i) -> p c t i", i=4),
+    )
+
+
+def tile_attend_plw_relu2_srt_kernel(tc, qT, k_words, k_scales, offs, out_0, out_1, out_2):
+    nc = tc.nc
+    with ExitStack() as ctx:
+        keep = ctx.enter_context(tc.tile_pool(name="keep", bufs=1))
+        psum = ctx.enter_context(tc.psum_pool(name="psum", bufs=1))
+
+        offsets = keep.tile([P, SLOTS // 16], U16, name="offsets")
+        nc.sync.dma_start(offsets[:], offs)
+
+        scale_pool = keep.tile([P, T], U8, name="scale_pool", align_bytes=64)
+        nc.sync.dma_start(
+            scale_pool[0:32, :].bitcast(I32), k_scales.rearrange("g f t -> (g f) t").bitcast(I32)
+        )
+        nc.vector.memset(scale_pool[32:64, :].bitcast(I32), 0)
+        nc.vector.memset(scale_pool[64:128, :].bitcast(I32), 0)
+        k_scale = keep.tile([P, PASSES * SLOTS], U8, name="k_scale", align_bytes=64)
+        nc.vector.memset(k_scale[:, SLOTS:].bitcast(I32), 0)
+
+        word_pool = keep.tile([P, T], I32, name="word_pool", align_bytes=64)
+        nc.scalar.dma_start(word_pool[:], k_words[0].rearrange("p t b -> p (t b)").bitcast(I32))
+
+        def load_q(g, first, width):
+            raw = keep.tile([P, PACK, width], F32, name="q_raw%d_%d" % (g, first), align_bytes=64)
+            rows = qT[0, 512 * g : 512 * (g + 1), first : first + width]
+            nc.scalar.dma_start(raw[:], rows.rearrange("(p j) w -> p j w", j=PACK))
+            return raw
+
+        q_first = load_q(0, 0, NQ)
+        q_second = [load_q(1, 0, HALF), load_q(1, HALF, HALF)]
+
+        scale_got = keep.tile([P, SLOTS], U8, name="scale_got", align_bytes=64)
+        nc.vector.tensor_copy(scale_got[:], scale_pool[:].indirect(offsets[:]))
+        nc.vector.tensor_copy(
+            k_scale[:, :SLOTS].rearrange("p (r s) -> p r s", r=PACK),
+            scale_got[:].rearrange("p (s r) -> p r s", r=PACK),
+        )
+        moves = [(g, quad) for g in range(PASSES) for quad in range(4) if (g, quad) != (0, 0)]
+        for g, quad in moves:
+            row = 16 * g + 4 * quad
+            queue = nc.gpsimd if (g, quad) in moves[-2:] else nc.sync
+            queue.dma_start(
+                k_scale[32 * quad : 32 * quad + 4, g * SLOTS : (g + 1) * SLOTS].bitcast(I32),
+                k_scale[row : row + 4, :SLOTS].bitcast(I32),
+            )
+
+        word_got = keep.tile([P, SLOTS], U32, name="word_got", align_bytes=64)
+        nc.vector.tensor_copy(word_got[:], word_pool[:].bitcast(U32).indirect(offsets[:]))
+        k_code = keep.tile([P, PASSES, PACK, P], U16, name="k_code", align_bytes=64)
+        nc.vector.tensor_copy(
+            k_code[:].rearrange("p g r (a b) -> p g a r b", b=4),
+            word_got[:].bitcast(U16).rearrange("p (a b r g) -> p g a r b", b=4, r=PACK, g=PASSES),
+        )
+
+        q_bf, q_code, q_scale = {}, {}, {}
+
+        def round_q(name, raw, width, on_scalar):
+            q_bf[name] = keep.tile([P, width, PACK], BF16, name="q_bf" + name, align_bytes=64)
+            dst, src = interleave_views(q_bf[name][:], raw)
+            if on_scalar:
+                nc.scalar.copy(dst, src)
+            else:
+                nc.vector.tensor_copy(dst, src)
+
+        def quantise_q(name, width, g, chunks):
+            code = keep.tile([P, width], U32, name="q_code" + name, align_bytes=64)
+            scale = keep.tile([P, width], U8, name="q_scale" + name, align_bytes=64)
+            nc.vector.quantize_mx(
+                out=code[:].bitcast(FP8X4),
+                scales=scale[:],
+                in_=q_bf[name][:].rearrange("p w j -> p (w j)"),
+            )
+            for i, c in enumerate(chunks):
+                q_code[g, c] = code[:, CHUNK * i : CHUNK * (i + 1)]
+                q_scale[g, c] = scale[:, CHUNK * i : CHUNK * (i + 1)]
+
+        y_code = keep.tile([P, NQ], U32, name="y_code", align_bytes=64)
+        y_scale = keep.tile([P, NQ], U8, name="y_scale", align_bytes=64)
+        out_rows = out_0.rearrange("(p r) q -> p r q", r=PACK)
+        out_words = out_1[0].rearrange("p q b -> p (q b)").bitcast(I32)
+        banks, relu, y, y_bf = {}, {}, {}, {}
+
+        def scores(c):
+            banks[c] = psum.tile([P, PACK, CHUNK], F32, name="bank%d" % c)
+            for r in range(PACK):
+                for g in range(PASSES):
+                    nc.tensor.matmul_mx(
+                        out=banks[c][:, r, :],
+                        lhsT=k_code[:, g, r, :].bitcast(FP4X4),
+                        lhsT_scale=k_scale[:, g * SLOTS + r * P : g * SLOTS + (r + 1) * P],
+                        rhs=q_code[g, c].bitcast(FP8X4),
+                        rhs_scale=q_scale[g, c],
+                        start=(g == 0),
+                        stop=(g == PASSES - 1),
+                    )
+
+        def weigh(c, relu_on_scalar):
+            relu[c] = keep.tile([P, PACK, CHUNK], F32, name="relu%d" % c)
+            if relu_on_scalar:
+                nc.scalar.activation(relu[c][:], banks[c][:], ACT.Relu)
+            else:
+                nc.vector.tensor_scalar_max(relu[c][:], banks[c][:], 0.0)
+            y[c] = keep.tile([P, PACK, CHUNK], F32, name="y%d" % c)
+            nc.scalar.activation(y[c][:], relu[c][:], ACT.Square)
+            nc.sync.dma_start(out_rows[:, :, CHUNK * c : CHUNK * (c + 1)], y[c][:])
+
+        def round_y(c):
+            y_bf[c] = keep.tile([P, CHUNK, PACK], BF16, name="y_bf%d" % c, align_bytes=64)
+            dst, src = interleave_views(y_bf[c][:], y[c][:])
+            nc.vector.tensor_copy(dst, src)
+
+        def quantise_y(c):
+            cols = slice(CHUNK * c, CHUNK * (c + 1))
+            nc.vector.quantize_mx(
+                out=y_code[:, cols].bitcast(FP8X4),
+                scales=y_scale[:, cols],
+                in_=y_bf[c][:].rearrange("p w j -> p (w j)"),
+            )
+
+        round_q("a", q_first[:, :, :HALF], HALF, False)
+        round_q("b", q_first[:, :, HALF:], HALF, True)
+        quantise_q("a", HALF, 0, (0, 1))
+        round_q("c", q_second[0][:, :, :CHUNK], CHUNK, False)
+        round_q("d", q_second[0][:, :, CHUNK:], CHUNK, True)
+        quantise_q("c", CHUNK, 1, (0,))
+        scores(0)
+        quantise_q("d", CHUNK, 1, (1,))
+        scores(1)
+        quantise_q("b", HALF, 0, (2, 3))
+        round_q("e", q_second[1][:], HALF, False)
+        weigh(0, True)
+        quantise_q("e", HALF, 1, (2, 3))
+        scores(2)
+        scores(3)
+        weigh(1, True)
+        round_y(0)
+        weigh(2, False)
+        quantise_y(0)
+        round_y(1)
+        weigh(3, True)
+        quantise_y(1)
+        nc.sync.dma_start(out_words[:, 0:HALF], y_code[:, 0:HALF].bitcast(I32))
+        round_y(2)
+        round_y(3)
+        quantise_y(2)
+        quantise_y(3)
+        nc.sync.dma_start(out_words[:, HALF:NQ], y_code[:, HALF:NQ].bitcast(I32))
+        for quad in range(4):
+            queue = nc.scalar if quad % 2 == 0 else nc.sync
+            queue.dma_start(
+                out_2[0, 4 * quad : 4 * quad + 4, :].bitcast(I32),
+                y_scale[32 * quad : 32 * quad + 4, :].bitcast(I32),
+            )

@@ -46,16 +46,20 @@ def tile_attend_plw_relu2_srt_kernel(tc, qT, k_words, k_scales, offs, out_0, out
         )
         nc.vector.memset(scale_pool[32:64, :].bitcast(I32), 0)
         nc.vector.memset(scale_pool[64:128, :].bitcast(I32), 0)
-        k_scale = keep.tile([P, PASSES * SLOTS], U8, name="k_scale", align_bytes=64)
-        nc.vector.memset(k_scale[:, SLOTS:].bitcast(I32), 0)
+        k_scale = [keep.tile([P, SLOTS], U8, name="k_scale%d" % g, align_bytes=64) for g in range(PASSES)]
+        nc.vector.memset(k_scale[1][:].bitcast(I32), 0)
+        warm_in = keep.tile([P, 8], F32, name="warm_in")
+        warm_out = keep.tile([P, 8], F32, name="warm_out")
+        nc.gpsimd.memset(warm_in[:], 0.0)
+        nc.scalar.activation(warm_out[:], warm_in[:], ACT.Relu)
 
         word_pool = keep.tile([P, T], I32, name="word_pool", align_bytes=64)
-        nc.scalar.dma_start(word_pool[:], k_words[0].rearrange("p t b -> p (t b)").bitcast(I32))
+        nc.sync.dma_start(word_pool[:], k_words[0].rearrange("p t b -> p (t b)").bitcast(I32))
 
         def load_q(g, first, width):
             raw = keep.tile([P, PACK, width], F32, name="q_raw%d_%d" % (g, first), align_bytes=64)
             rows = qT[0, 512 * g : 512 * (g + 1), first : first + width]
-            nc.scalar.dma_start(raw[:], rows.rearrange("(p j) w -> p j w", j=PACK))
+            nc.sync.dma_start(raw[:], rows.rearrange("(p j) w -> p j w", j=PACK))
             return raw
 
         q_first = load_q(0, 0, NQ)
@@ -64,16 +68,16 @@ def tile_attend_plw_relu2_srt_kernel(tc, qT, k_words, k_scales, offs, out_0, out
         scale_got = keep.tile([P, SLOTS], U8, name="scale_got", align_bytes=64)
         nc.vector.tensor_copy(scale_got[:], scale_pool[:].indirect(offsets[:]))
         nc.vector.tensor_copy(
-            k_scale[:, :SLOTS].rearrange("p (r s) -> p r s", r=PACK),
+            k_scale[0][:].rearrange("p (r s) -> p r s", r=PACK),
             scale_got[:].rearrange("p (s r) -> p r s", r=PACK),
         )
         moves = [(g, quad) for g in range(PASSES) for quad in range(4) if (g, quad) != (0, 0)]
         for g, quad in moves:
             row = 16 * g + 4 * quad
-            queue = nc.gpsimd if (g, quad) in moves[-2:] else nc.sync
+            queue = nc.gpsimd if (g, quad) == moves[-1] else nc.scalar
             queue.dma_start(
-                k_scale[32 * quad : 32 * quad + 4, g * SLOTS : (g + 1) * SLOTS].bitcast(I32),
-                k_scale[row : row + 4, :SLOTS].bitcast(I32),
+                k_scale[g][32 * quad : 32 * quad + 4, :].bitcast(I32),
+                k_scale[0][row : row + 4, :].bitcast(I32),
             )
 
         word_got = keep.tile([P, SLOTS], U32, name="word_got", align_bytes=64)
@@ -112,26 +116,34 @@ def tile_attend_plw_relu2_srt_kernel(tc, qT, k_words, k_scales, offs, out_0, out
         out_words = out_1[0].rearrange("p q b -> p (q b)").bitcast(I32)
         banks, relu, y, y_bf = {}, {}, {}, {}
 
-        def scores(c):
-            banks[c] = psum.tile([P, PACK, CHUNK], F32, name="bank%d" % c)
-            for r in range(PACK):
-                for g in range(PASSES):
-                    nc.tensor.matmul_mx(
-                        out=banks[c][:, r, :],
-                        lhsT=k_code[:, g, r, :].bitcast(FP4X4),
-                        lhsT_scale=k_scale[:, g * SLOTS + r * P : g * SLOTS + (r + 1) * P],
-                        rhs=q_code[g, c].bitcast(FP8X4),
-                        rhs_scale=q_scale[g, c],
-                        start=(g == 0),
-                        stop=(g == PASSES - 1),
-                    )
+        def score_pass(c, r, g):
+            nc.tensor.matmul_mx(
+                out=banks[c, r // 2][:, r % 2, :],
+                lhsT=k_code[:, g, r, :].bitcast(FP4X4),
+                lhsT_scale=k_scale[g][:, r * P : (r + 1) * P],
+                rhs=q_code[g, c].bitcast(FP8X4),
+                rhs_scale=q_scale[g, c],
+                start=(g == 0),
+                stop=(g == PASSES - 1),
+            )
 
-        def weigh(c, relu_on_scalar):
+        def open_scores(c):
+            for pair in range(2):
+                banks[c, pair] = psum.tile([P, 2, CHUNK], F32, name="bank%d_%d" % (c, pair))
+                score_pass(c, 2 * pair, 0)
+
+        def close_scores(c):
+            for pair in range(2):
+                score_pass(c, 2 * pair, 1)
+                score_pass(c, 2 * pair + 1, 0)
+                score_pass(c, 2 * pair + 1, 1)
+
+        def rectify(c):
             relu[c] = keep.tile([P, PACK, CHUNK], F32, name="relu%d" % c)
-            if relu_on_scalar:
-                nc.scalar.activation(relu[c][:], banks[c][:], ACT.Relu)
-            else:
-                nc.vector.tensor_scalar_max(relu[c][:], banks[c][:], 0.0)
+            nc.scalar.activation(relu[c][:, 0:2, :], banks[c, 0][:], ACT.Relu)
+            nc.vector.tensor_scalar_max(relu[c][:, 2:4, :], banks[c, 1][:], 0.0)
+
+        def square(c):
             y[c] = keep.tile([P, PACK, CHUNK], F32, name="y%d" % c)
             nc.scalar.activation(y[c][:], relu[c][:], ACT.Square)
             nc.sync.dma_start(out_rows[:, :, CHUNK * c : CHUNK * (c + 1)], y[c][:])
@@ -152,31 +164,41 @@ def tile_attend_plw_relu2_srt_kernel(tc, qT, k_words, k_scales, offs, out_0, out
         round_q("a", q_first[:, :, :HALF], HALF, False)
         round_q("b", q_first[:, :, HALF:], HALF, True)
         quantise_q("a", HALF, 0, (0, 1))
+        open_scores(0)
+        open_scores(1)
         round_q("c", q_second[0][:, :, :CHUNK], CHUNK, False)
         round_q("d", q_second[0][:, :, CHUNK:], CHUNK, True)
-        quantise_q("c", CHUNK, 1, (0,))
-        scores(0)
-        quantise_q("d", CHUNK, 1, (1,))
-        scores(1)
         quantise_q("b", HALF, 0, (2, 3))
-        round_q("e", q_second[1][:], HALF, False)
-        weigh(0, True)
-        quantise_q("e", HALF, 1, (2, 3))
-        scores(2)
-        scores(3)
-        weigh(1, True)
+        quantise_q("c", CHUNK, 1, (0,))
+        open_scores(2)
+        open_scores(3)
+        close_scores(0)
+        round_q("e", q_second[1][:, :, :CHUNK], CHUNK, True)
+        quantise_q("d", CHUNK, 1, (1,))
+        close_scores(1)
+        round_q("f", q_second[1][:, :, CHUNK:], CHUNK, False)
+        quantise_q("e", CHUNK, 1, (2,))
+        close_scores(2)
+        quantise_q("f", CHUNK, 1, (3,))
+        close_scores(3)
+        rectify(0)
+        square(0)
+        rectify(1)
         round_y(0)
-        weigh(2, False)
+        square(1)
+        rectify(2)
         quantise_y(0)
         round_y(1)
-        weigh(3, True)
+        square(2)
+        rectify(3)
         quantise_y(1)
-        nc.sync.dma_start(out_words[:, 0:HALF], y_code[:, 0:HALF].bitcast(I32))
         round_y(2)
-        round_y(3)
+        square(3)
         quantise_y(2)
+        nc.sync.dma_start(out_words[:, : 3 * CHUNK], y_code[:, : 3 * CHUNK].bitcast(I32))
+        round_y(3)
         quantise_y(3)
-        nc.sync.dma_start(out_words[:, HALF:NQ], y_code[:, HALF:NQ].bitcast(I32))
+        nc.sync.dma_start(out_words[:, 3 * CHUNK :], y_code[:, 3 * CHUNK :].bitcast(I32))
         for quad in range(4):
             queue = nc.scalar if quad % 2 == 0 else nc.sync
             queue.dma_start(

@@ -48,10 +48,6 @@ def tile_attend_plw_relu2_srt_kernel(tc, qT, k_words, k_scales, offs, out_0, out
         nc.vector.memset(scale_pool[64:128, :].bitcast(I32), 0)
         k_scale = [keep.tile([P, SLOTS], U8, name="k_scale%d" % g, align_bytes=64) for g in range(PASSES)]
         nc.vector.memset(k_scale[1][:].bitcast(I32), 0)
-        warm_in = keep.tile([P, 8], F32, name="warm_in")
-        warm_out = keep.tile([P, 8], F32, name="warm_out")
-        nc.gpsimd.memset(warm_in[:], 0.0)
-        nc.scalar.activation(warm_out[:], warm_in[:], ACT.Relu)
 
         word_pool = keep.tile([P, T], I32, name="word_pool", align_bytes=64)
         nc.sync.dma_start(word_pool[:], k_words[0].rearrange("p t b -> p (t b)").bitcast(I32))
@@ -63,7 +59,6 @@ def tile_attend_plw_relu2_srt_kernel(tc, qT, k_words, k_scales, offs, out_0, out
             return raw
 
         q_first = load_q(0, 0, NQ)
-        q_second = [load_q(1, 0, HALF), load_q(1, HALF, HALF)]
 
         scale_got = keep.tile([P, SLOTS], U8, name="scale_got", align_bytes=64)
         nc.vector.tensor_copy(scale_got[:], scale_pool[:].indirect(offsets[:]))
@@ -71,14 +66,18 @@ def tile_attend_plw_relu2_srt_kernel(tc, qT, k_words, k_scales, offs, out_0, out
             k_scale[0][:].rearrange("p (r s) -> p r s", r=PACK),
             scale_got[:].rearrange("p (s r) -> p r s", r=PACK),
         )
-        moves = [(g, quad) for g in range(PASSES) for quad in range(4) if (g, quad) != (0, 0)]
-        for g, quad in moves:
-            row = 16 * g + 4 * quad
-            queue = nc.gpsimd if (g, quad) == moves[-1] else nc.scalar
-            queue.dma_start(
-                k_scale[g][32 * quad : 32 * quad + 4, :].bitcast(I32),
-                k_scale[0][row : row + 4, :].bitcast(I32),
-            )
+
+        def move_scale_rows(g, quads):
+            for quad in quads:
+                row = 16 * g + 4 * quad
+                nc.sync.dma_start(
+                    k_scale[g][32 * quad : 32 * quad + 4, :].bitcast(I32),
+                    k_scale[0][row : row + 4, :].bitcast(I32),
+                )
+
+        move_scale_rows(0, (1, 2, 3))
+        q_second = [load_q(1, 0, HALF), load_q(1, HALF, HALF)]
+        move_scale_rows(1, (0, 1, 2, 3))
 
         word_got = keep.tile([P, SLOTS], U32, name="word_got", align_bytes=64)
         nc.vector.tensor_copy(word_got[:], word_pool[:].bitcast(U32).indirect(offsets[:]))
@@ -114,11 +113,11 @@ def tile_attend_plw_relu2_srt_kernel(tc, qT, k_words, k_scales, offs, out_0, out
         y_scale = keep.tile([P, NQ], U8, name="y_scale", align_bytes=64)
         out_rows = out_0.rearrange("(p r) q -> p r q", r=PACK)
         out_words = out_1[0].rearrange("p q b -> p (q b)").bitcast(I32)
-        banks, relu, y, y_bf = {}, {}, {}, {}
+        banks, whole_banks, relu, y, y_bf = {}, {}, {}, {}, {}
 
         def score_pass(c, r, g):
             nc.tensor.matmul_mx(
-                out=banks[c, r // 2][:, r % 2, :],
+                out=banks[c, r],
                 lhsT=k_code[:, g, r, :].bitcast(FP4X4),
                 lhsT_scale=k_scale[g][:, r * P : (r + 1) * P],
                 rhs=q_code[g, c].bitcast(FP8X4),
@@ -127,21 +126,23 @@ def tile_attend_plw_relu2_srt_kernel(tc, qT, k_words, k_scales, offs, out_0, out
                 stop=(g == PASSES - 1),
             )
 
-        def open_scores(c):
-            for pair in range(2):
-                banks[c, pair] = psum.tile([P, 2, CHUNK], F32, name="bank%d_%d" % (c, pair))
-                score_pass(c, 2 * pair, 0)
+        def take_banks(c, tags):
+            per_bank = PACK // len(tags)
+            for b, tag in enumerate(tags):
+                bank = psum.tile([P, per_bank, CHUNK], F32, name="bank%d_%d" % (c, b), tag="bank%d" % tag)
+                whole_banks[c, b] = bank
+                for i in range(per_bank):
+                    banks[c, per_bank * b + i] = bank[:, i, :]
 
-        def close_scores(c):
-            for pair in range(2):
-                score_pass(c, 2 * pair, 1)
-                score_pass(c, 2 * pair + 1, 0)
-                score_pass(c, 2 * pair + 1, 1)
-
-        def rectify(c):
+        def rectify(c, count):
             relu[c] = keep.tile([P, PACK, CHUNK], F32, name="relu%d" % c)
-            nc.scalar.activation(relu[c][:, 0:2, :], banks[c, 0][:], ACT.Relu)
-            nc.vector.tensor_scalar_max(relu[c][:, 2:4, :], banks[c, 1][:], 0.0)
+            per_bank = PACK // count
+            for b in range(count):
+                dst = relu[c][:, per_bank * b : per_bank * (b + 1), :]
+                if b < count // 2:
+                    nc.scalar.activation(dst, whole_banks[c, b][:], ACT.Relu)
+                else:
+                    nc.vector.tensor_scalar_max(dst, whole_banks[c, b][:], 0.0)
 
         def square(c):
             y[c] = keep.tile([P, PACK, CHUNK], F32, name="y%d" % c)
@@ -164,33 +165,45 @@ def tile_attend_plw_relu2_srt_kernel(tc, qT, k_words, k_scales, offs, out_0, out
         round_q("a", q_first[:, :, :HALF], HALF, False)
         round_q("b", q_first[:, :, HALF:], HALF, True)
         quantise_q("a", HALF, 0, (0, 1))
-        open_scores(0)
-        open_scores(1)
+        take_banks(0, (0, 1, 2, 3))
+        take_banks(1, (4, 5))
+        for r in range(PACK):
+            score_pass(0, r, 0)
+        for r in (0, 2):
+            score_pass(1, r, 0)
         round_q("c", q_second[0][:, :, :CHUNK], CHUNK, False)
         round_q("d", q_second[0][:, :, CHUNK:], CHUNK, True)
         quantise_q("b", HALF, 0, (2, 3))
         quantise_q("c", CHUNK, 1, (0,))
-        open_scores(2)
-        open_scores(3)
-        close_scores(0)
+        for r in range(PACK):
+            score_pass(0, r, 1)
         round_q("e", q_second[1][:, :, :CHUNK], CHUNK, True)
         quantise_q("d", CHUNK, 1, (1,))
-        close_scores(1)
+        for r in (0, 2):
+            score_pass(1, r, 1)
+            score_pass(1, r + 1, 0)
+            score_pass(1, r + 1, 1)
         round_q("f", q_second[1][:, :, CHUNK:], CHUNK, False)
         quantise_q("e", CHUNK, 1, (2,))
-        close_scores(2)
         quantise_q("f", CHUNK, 1, (3,))
-        close_scores(3)
-        rectify(0)
+        take_banks(2, (6, 7))
+        for r in range(PACK):
+            for g in range(PASSES):
+                score_pass(2, r, g)
+        rectify(0, 4)
+        take_banks(3, (0, 2))
+        for r in range(PACK):
+            for g in range(PASSES):
+                score_pass(3, r, g)
         square(0)
-        rectify(1)
+        rectify(1, 2)
         round_y(0)
         square(1)
-        rectify(2)
+        rectify(2, 2)
         quantise_y(0)
         round_y(1)
         square(2)
-        rectify(3)
+        rectify(3, 2)
         quantise_y(1)
         round_y(2)
         square(3)

@@ -134,39 +134,52 @@ def tile_attend_plw_relu2_srt_kernel(tc, qT, k_words, k_scales, offs, out_0, out
                 for i in range(per_bank):
                     banks[c, per_bank * b + i] = bank[:, i, :]
 
-        def rectify(c, count):
-            relu[c] = keep.tile([P, PACK, CHUNK], F32, name="relu%d" % c)
-            per_bank = PACK // count
-            for b in range(count):
-                dst = relu[c][:, per_bank * b : per_bank * (b + 1), :]
-                if b < count // 2:
-                    nc.scalar.activation(dst, whole_banks[c, b][:], ACT.Relu)
+        def rectify(c, pair, on_scalar, tag):
+            relu[c, pair] = keep.tile([P, 2, CHUNK], F32, name="relu%d_%d" % (c, pair), tag=tag, align_bytes=64)
+            if c == 0:
+                parts = [(relu[c, pair][:, i, :], whole_banks[c, 2 * pair + i][:, 0, :]) for i in range(2)]
+            else:
+                parts = [(relu[c, pair][:], whole_banks[c, pair][:])]
+            for dst, src in parts:
+                if on_scalar:
+                    nc.scalar.activation(dst, src, ACT.Relu)
                 else:
-                    nc.vector.tensor_scalar_max(dst, whole_banks[c, b][:], 0.0)
+                    nc.vector.tensor_scalar_max(dst, src, 0.0)
 
-        def square(c):
-            y[c] = keep.tile([P, PACK, CHUNK], F32, name="y%d" % c)
-            nc.scalar.activation(y[c][:], relu[c][:], ACT.Square)
+        def square(c, pair, cols):
+            nc.scalar.activation(y[c][:, 2 * pair : 2 * pair + 2, cols], relu[c, pair][:, :, cols], ACT.Square)
+
+        def store_y(c):
             nc.sync.dma_start(out_rows[:, :, CHUNK * c : CHUNK * (c + 1)], y[c][:])
 
-        def round_y(c):
-            y_bf[c] = keep.tile([P, CHUNK, PACK], BF16, name="y_bf%d" % c, align_bytes=64)
-            dst, src = interleave_views(y_bf[c][:], y[c][:])
+        def round_y(c, cols, tag):
+            width = cols.stop - cols.start
+            y_bf[c, cols.start] = keep.tile(
+                [P, width, PACK], BF16, name="y_bf%d_%d" % (c, cols.start), tag=tag, align_bytes=64
+            )
+            dst, src = interleave_views(y_bf[c, cols.start][:], y[c][:, :, cols])
             nc.vector.tensor_copy(dst, src)
 
-        def quantise_y(c):
-            cols = slice(CHUNK * c, CHUNK * (c + 1))
+        def quantise_y(c, cols):
+            at = slice(CHUNK * c + cols.start, CHUNK * c + cols.stop)
             nc.vector.quantize_mx(
-                out=y_code[:, cols].bitcast(FP8X4),
-                scales=y_scale[:, cols],
-                in_=y_bf[c][:].rearrange("p w j -> p (w j)"),
+                out=y_code[:, at].bitcast(FP8X4),
+                scales=y_scale[:, at],
+                in_=y_bf[c, cols.start][:].rearrange("p w j -> p (w j)"),
             )
 
-        round_q("a", q_first[:, :, :HALF], HALF, False)
+        for c in range(4):
+            y[c] = keep.tile([P, PACK, CHUNK], F32, name="y%d" % c)
+        whole, low, high = slice(0, CHUNK), slice(0, CHUNK // 2), slice(CHUNK // 2, CHUNK)
+
+        round_q("a0", q_first[:, :, :CHUNK], CHUNK, False)
+        round_q("a1", q_first[:, :, CHUNK:HALF], CHUNK, False)
         round_q("b", q_first[:, :, HALF:], HALF, True)
-        quantise_q("a", HALF, 0, (0, 1))
+        quantise_q("a0", CHUNK, 0, (0,))
+        quantise_q("a1", CHUNK, 0, (1,))
         take_banks(0, (0, 1, 2, 3))
         take_banks(1, (4, 5))
+        take_banks(2, (6, 7))
         for r in range(PACK):
             score_pass(0, r, 0)
         for r in (0, 2):
@@ -174,43 +187,57 @@ def tile_attend_plw_relu2_srt_kernel(tc, qT, k_words, k_scales, offs, out_0, out
         round_q("c", q_second[0][:, :, :CHUNK], CHUNK, False)
         round_q("d", q_second[0][:, :, CHUNK:], CHUNK, True)
         quantise_q("b", HALF, 0, (2, 3))
+        for r in (0, 2):
+            score_pass(2, r, 0)
         quantise_q("c", CHUNK, 1, (0,))
         for r in range(PACK):
             score_pass(0, r, 1)
         round_q("e", q_second[1][:, :, :CHUNK], CHUNK, True)
         quantise_q("d", CHUNK, 1, (1,))
-        for r in (0, 2):
-            score_pass(1, r, 1)
-            score_pass(1, r + 1, 0)
-            score_pass(1, r + 1, 1)
         round_q("f", q_second[1][:, :, CHUNK:], CHUNK, False)
         quantise_q("e", CHUNK, 1, (2,))
         quantise_q("f", CHUNK, 1, (3,))
-        take_banks(2, (6, 7))
-        for r in range(PACK):
-            for g in range(PASSES):
-                score_pass(2, r, g)
-        rectify(0, 4)
+        for c in (1, 2):
+            for r in (0, 2):
+                score_pass(c, r, 1)
+                score_pass(c, r + 1, 0)
+                score_pass(c, r + 1, 1)
+        rectify(0, 0, True, "relu00")
+        rectify(0, 1, False, "relu01")
         take_banks(3, (0, 2))
         for r in range(PACK):
             for g in range(PASSES):
                 score_pass(3, r, g)
-        square(0)
-        rectify(1, 2)
-        round_y(0)
-        square(1)
-        rectify(2, 2)
-        quantise_y(0)
-        round_y(1)
-        square(2)
-        rectify(3, 2)
-        quantise_y(1)
-        round_y(2)
-        square(3)
-        quantise_y(2)
+        square(0, 0, whole)
+        square(0, 1, whole)
+        store_y(0)
+        rectify(1, 0, False, "relu10")
+        rectify(1, 1, False, "relu11")
+        round_y(0, whole, "ybf0")
+        rectify(2, 0, True, "relu01")
+        rectify(2, 1, False, "relu21")
+        square(1, 0, whole)
+        square(1, 1, whole)
+        store_y(1)
+        quantise_y(0, whole)
+        rectify(3, 0, True, "relu10")
+        rectify(3, 1, False, "ybf0")
+        round_y(1, whole, "ybf1")
+        square(2, 0, whole)
+        square(2, 1, whole)
+        store_y(2)
+        quantise_y(1, whole)
+        round_y(2, whole, "ybf2")
+        for cols in (low, high):
+            square(3, 0, cols)
+            square(3, 1, cols)
+        store_y(3)
+        quantise_y(2, whole)
         nc.sync.dma_start(out_words[:, : 3 * CHUNK], y_code[:, : 3 * CHUNK].bitcast(I32))
-        round_y(3)
-        quantise_y(3)
+        round_y(3, low, "ybf3")
+        round_y(3, high, "ybf4")
+        quantise_y(3, low)
+        quantise_y(3, high)
         nc.sync.dma_start(out_words[:, 3 * CHUNK :], y_code[:, 3 * CHUNK :].bitcast(I32))
         for quad in range(4):
             queue = nc.scalar if quad % 2 == 0 else nc.sync

from contextlib import ExitStack

import concourse.mybir as mybir

F32 = mybir.dt.float32
BF16 = mybir.dt.bfloat16
I32 = mybir.dt.int32
U32 = mybir.dt.uint32
U16 = mybir.dt.uint16
U8 = mybir.dt.uint8
FP8X4 = mybir.dt.float8_e4m3fn_x4
FP4X4 = mybir.dt.float4_e2m1fn_x4
ACT = mybir.ActivationFunctionType
ALU = mybir.AluOpType

P = 128
PACK = 4
PASSES = 2
T = 2048
SLOTS = 512
NQ = 512
HALF = 256
CHUNK = 128
FLOPS = 2 * SLOTS * NQ * 1024


def interleave_views(dst, src):
    return (
        dst.rearrange("p (c i) t -> p c t i", i=4),
        src.rearrange("p t (c i) -> p c t i", i=4),
    )


def tile_attend_plw_relu2_srt_kernel(tc, qT, k_words, k_scales, offs, out_0, out_1, out_2):
    nc = tc.nc
    with ExitStack() as ctx:
        keep = ctx.enter_context(tc.tile_pool(name="keep", bufs=1))
        psum = ctx.enter_context(tc.psum_pool(name="psum", bufs=1))

        offsets = keep.tile([P, SLOTS // 16], U16, name="offsets")
        nc.sync.dma_start(offsets[:], offs)

        scale_pool = keep.tile([P, T], U8, name="scale_pool", align_bytes=64)
        nc.sync.dma_start(
            scale_pool[0:32, :].bitcast(I32), k_scales.rearrange("g f t -> (g f) t").bitcast(I32)
        )
        nc.vector.memset(scale_pool[32:64, :].bitcast(I32), 0)
        nc.vector.memset(scale_pool[64:128, :].bitcast(I32), 0)
        k_scale = [keep.tile([P, SLOTS], U8, name="k_scale%d" % g, align_bytes=64) for g in range(PASSES)]
        nc.vector.memset(k_scale[1][:].bitcast(I32), 0)

        word_pool = keep.tile([P, T], I32, name="word_pool", align_bytes=64)
        nc.sync.dma_start(word_pool[:], k_words[0].rearrange("p t b -> p (t b)").bitcast(I32))

        def load_q(g, first, width):
            raw = keep.tile([P, PACK, width], F32, name="q_raw%d_%d" % (g, first), align_bytes=64)
            rows = qT[0, 512 * g : 512 * (g + 1), first : first + width]
            nc.sync.dma_start(raw[:], rows.rearrange("(p j) w -> p j w", j=PACK))
            return raw

        q_first = load_q(0, 0, NQ)

        scale_got = keep.tile([P, SLOTS], U8, name="scale_got", align_bytes=64)
        nc.vector.tensor_copy(scale_got[:], scale_pool[:].indirect(offsets[:]))
        nc.vector.tensor_copy(
            k_scale[0][:].rearrange("p (r s) -> p r s", r=PACK),
            scale_got[:].rearrange("p (s r) -> p r s", r=PACK),
        )

        def move_scale_rows(g, quads):
            for quad in quads:
                row = 16 * g + 4 * quad
                nc.sync.dma_start(
                    k_scale[g][32 * quad : 32 * quad + 4, :].bitcast(I32),
                    k_scale[0][row : row + 4, :].bitcast(I32),
                )

        move_scale_rows(0, (1, 2, 3))
        q_second = [load_q(1, 0, HALF), load_q(1, HALF, HALF)]
        move_scale_rows(1, (0, 1, 2, 3))

        word_got = keep.tile([P, SLOTS], U32, name="word_got", align_bytes=64)
        nc.vector.tensor_copy(word_got[:], word_pool[:].bitcast(U32).indirect(offsets[:]))
        k_code = keep.tile([P, PASSES, PACK, P], U16, name="k_code", align_bytes=64)
        nc.vector.tensor_copy(
            k_code[:].rearrange("p g r (a b) -> p g a r b", b=4),
            word_got[:].bitcast(U16).rearrange("p (a b r g) -> p g a r b", b=4, r=PACK, g=PASSES),
        )

        q_bf, q_code, q_scale = {}, {}, {}

        def round_q(name, raw, width, on_scalar):
            q_bf[name] = keep.tile([P, width, PACK], BF16, name="q_bf" + name, align_bytes=64)
            dst, src = interleave_views(q_bf[name][:], raw)
            if on_scalar:
                nc.scalar.copy(dst, src)
            else:
                nc.vector.tensor_copy(dst, src)

        def quantise_q(name, width, g, chunks):
            code = keep.tile([P, width], U32, name="q_code" + name, align_bytes=64)
            scale = keep.tile([P, width], U8, name="q_scale" + name, align_bytes=64)
            nc.vector.quantize_mx(
                out=code[:].bitcast(FP8X4),
                scales=scale[:],
                in_=q_bf[name][:].rearrange("p w j -> p (w j)"),
            )
            for i, c in enumerate(chunks):
                q_code[g, c] = code[:, CHUNK * i : CHUNK * (i + 1)]
                q_scale[g, c] = scale[:, CHUNK * i : CHUNK * (i + 1)]

        y_code = keep.tile([P, NQ], U32, name="y_code", align_bytes=64)
        y_scale = keep.tile([P, NQ], U8, name="y_scale", align_bytes=64)
        out_rows = out_0.rearrange("(p r) q -> p r q", r=PACK)
        out_words = out_1[0].rearrange("p q b -> p (q b)").bitcast(I32)
        banks, whole_banks, relu, y, y_bf = {}, {}, {}, {}, {}

        def score_pass(c, r, g):
            nc.tensor.matmul_mx(
                out=banks[c, r],
                lhsT=k_code[:, g, r, :].bitcast(FP4X4),
                lhsT_scale=k_scale[g][:, r * P : (r + 1) * P],
                rhs=q_code[g, c].bitcast(FP8X4),
                rhs_scale=q_scale[g, c],
                start=(g == 0),
                stop=(g == PASSES - 1),
            )

        def take_banks(c, tags):
            per_bank = PACK // len(tags)
            for b, tag in enumerate(tags):
                bank = psum.tile([P, per_bank, CHUNK], F32, name="bank%d_%d" % (c, b), tag="bank%d" % tag)
                whole_banks[c, b] = bank
                for i in range(per_bank):
                    banks[c, per_bank * b + i] = bank[:, i, :]

        def rectify(c, pair, on_scalar, tag):
            relu[c, pair] = keep.tile([P, 2, CHUNK], F32, name="relu%d_%d" % (c, pair), tag=tag, align_bytes=64)
            if c == 0:
                parts = [(relu[c, pair][:, i, :], whole_banks[c, 2 * pair + i][:, 0, :]) for i in range(2)]
            else:
                parts = [(relu[c, pair][:], whole_banks[c, pair][:])]
            for dst, src in parts:
                if on_scalar:
                    nc.scalar.activation(dst, src, ACT.Relu)
                else:
                    nc.vector.tensor_scalar_max(dst, src, 0.0)

        def square(c, pair, cols):
            nc.scalar.activation(y[c][:, 2 * pair : 2 * pair + 2, cols], relu[c, pair][:, :, cols], ACT.Square)

        def store_y(c):
            nc.sync.dma_start(out_rows[:, :, CHUNK * c : CHUNK * (c + 1)], y[c][:])

        def round_y(c, cols, tag):
            width = cols.stop - cols.start
            y_bf[c, cols.start] = keep.tile(
                [P, width, PACK], BF16, name="y_bf%d_%d" % (c, cols.start), tag=tag, align_bytes=64
            )
            dst, src = interleave_views(y_bf[c, cols.start][:], y[c][:, :, cols])
            nc.vector.tensor_copy(dst, src)

        def quantise_y(c, cols):
            at = slice(CHUNK * c + cols.start, CHUNK * c + cols.stop)
            nc.vector.quantize_mx(
                out=y_code[:, at].bitcast(FP8X4),
                scales=y_scale[:, at],
                in_=y_bf[c, cols.start][:].rearrange("p w j -> p (w j)"),
            )

        for c in range(4):
            y[c] = keep.tile([P, PACK, CHUNK], F32, name="y%d" % c)
        whole, low, high = slice(0, CHUNK), slice(0, CHUNK // 2), slice(CHUNK // 2, CHUNK)

        round_q("a0", q_first[:, :, :CHUNK], CHUNK, False)
        round_q("a1", q_first[:, :, CHUNK:HALF], CHUNK, False)
        round_q("b", q_first[:, :, HALF:], HALF, True)
        quantise_q("a0", CHUNK, 0, (0,))
        quantise_q("a1", CHUNK, 0, (1,))
        take_banks(0, (0, 1, 2, 3))
        take_banks(1, (4, 5))
        take_banks(2, (6, 7))
        for r in range(PACK):
            score_pass(0, r, 0)
        for r in (0, 2):
            score_pass(1, r, 0)
        round_q("c", q_second[0][:, :, :CHUNK], CHUNK, False)
        round_q("d", q_second[0][:, :, CHUNK:], CHUNK, True)
        quantise_q("b", HALF, 0, (2, 3))
        for r in (0, 2):
            score_pass(2, r, 0)
        quantise_q("c", CHUNK, 1, (0,))
        for r in range(PACK):
            score_pass(0, r, 1)
        round_q("e", q_second[1][:, :, :CHUNK], CHUNK, True)
        quantise_q("d", CHUNK, 1, (1,))
        round_q("f", q_second[1][:, :, CHUNK:], CHUNK, False)
        quantise_q("e", CHUNK, 1, (2,))
        quantise_q("f", CHUNK, 1, (3,))
        for c in (1, 2):
            for r in (0, 2):
                score_pass(c, r, 1)
                score_pass(c, r + 1, 0)
                score_pass(c, r + 1, 1)
        rectify(0, 0, True, "relu00")
        rectify(0, 1, False, "relu01")
        take_banks(3, (0, 2))
        for r in range(PACK):
            for g in range(PASSES):
                score_pass(3, r, g)
        square(0, 0, whole)
        square(0, 1, whole)
        store_y(0)
        rectify(1, 0, False, "relu10")
        rectify(1, 1, False, "relu11")
        round_y(0, whole, "ybf0")
        rectify(2, 0, True, "relu01")
        rectify(2, 1, False, "relu21")
        square(1, 0, whole)
        square(1, 1, whole)
        store_y(1)
        quantise_y(0, whole)
        rectify(3, 0, True, "relu10")
        rectify(3, 1, False, "ybf0")
        round_y(1, whole, "ybf1")
        square(2, 0, whole)
        square(2, 1, whole)
        store_y(2)
        quantise_y(1, whole)
        round_y(2, whole, "ybf2")
        for cols in (low, high):
            square(3, 0, cols)
            square(3, 1, cols)
        store_y(3)
        quantise_y(2, whole)
        nc.sync.dma_start(out_words[:, : 3 * CHUNK], y_code[:, : 3 * CHUNK].bitcast(I32))
        round_y(3, low, "ybf3")
        round_y(3, high, "ybf4")
        quantise_y(3, low)
        quantise_y(3, high)
        nc.sync.dma_start(out_words[:, 3 * CHUNK :], y_code[:, 3 * CHUNK :].bitcast(I32))
        for quad in range(4):
            queue = nc.scalar if quad % 2 == 0 else nc.sync
            queue.dma_start(
                out_2[0, 4 * quad : 4 * quad + 4, :].bitcast(I32),
                y_scale[32 * quad : 32 * quad + 4, :].bitcast(I32),
            )
